import numpy as np
import ml_dtypes


def mxq(x, axis, fmt="e4m3"):
    dtype, down = {"e4m3": (ml_dtypes.float8_e4m3fn, 7), "e5m2": (ml_dtypes.float8_e5m2, 14)}[fmt]
    v = np.moveaxis(np.asarray(x, np.float32).astype(ml_dtypes.bfloat16).astype(np.float64), axis, -1)
    blocks = v.reshape(v.shape[:-1] + (-1, 32))
    amax = np.abs(blocks).max(-1, keepdims=True)
    byte = np.maximum(np.where(amax > 0, np.frexp(amax)[1] - 1 + 127, 0) - down, 1)
    scale = np.exp2(byte - 127.0)
    codes = (blocks / scale).astype(np.float32).astype(dtype).astype(np.float64)
    return np.moveaxis((codes * scale).reshape(v.shape), -1, axis)


WIDE = False


def mx_kscale(k, group=512):
    if not WIDE:
        return np.ones(k)
    levels = np.array([18, -18])
    if group != 512:
        return np.exp2(np.random.permutation(np.resize(levels, k // group))).repeat(group)
    if k % 512:
        return np.exp2(np.random.permutation(np.resize(levels, k // 32))).repeat(32)
    a = np.empty((k // 512, 16))
    for p in range(k // 512):
        a[p, :8] = np.random.permutation(np.resize(levels, 8))
        for g in range(8):
            far = levels[np.abs(levels - a[p, g]) >= 10]
            a[p, g + 8] = far[np.random.randint(len(far))]
    return np.exp2(a.ravel()).repeat(32)


def f64(x):
    return np.asarray(x).astype(np.float64)


G, D, M, O, N = 4, 128, 128, 128, 512


def setup_inputs():
    n = np.random.standard_normal
    s_d = mx_kscale(D, 0)
    s_o = mx_kscale(O, 0)
    return {
        "x": (n((G, D, N)) * s_d[:, None]).astype(np.float32),
        "w1": (n((G, D, M)) / np.sqrt(D) / s_d[:, None]).astype(np.float32),
        "w2": (n((G, D, M)) / np.sqrt(D) / s_d[:, None]).astype(np.float32),
        "sh": (np.random.uniform(0.1, 0.4, (G, M, 1))).astype(np.float32),
        "d0": (np.random.uniform(2.0, 6.0, (G, M, N))).astype(np.float32),
        "wo": (n((G, O, M)) / np.sqrt(O) / s_o[:, None]).astype(np.float32),
        "dy": (n((G, O, N)) * s_o[:, None]).astype(np.float32),
        "old": (0.3 * n((G, M, N))).astype(np.float32),
    }


def reference(x, w1, w2, sh, d0, wo, dy, old):
    w1q = mxq(f64(w1), 1, "e4m3")
    xq = mxq(f64(x), 1, "e4m3")
    z1 = w1q.transpose(0, 2, 1) @ xq
    w2q = mxq(f64(w2), 1, "e4m3")
    z2 = w2q.transpose(0, 2, 1) @ xq
    q1 = f64(d0) - z1 * 2.0
    woq = mxq(f64(wo), 1, "e4m3")
    dyq = mxq(f64(dy), 1, "e4m3")
    c0 = woq.transpose(0, 2, 1) @ dyq
    dq1 = c0 * z2 * np.exp(q1 * f64(sh) * (-1.0)) * (-1.0) * f64(sh)
    dz1 = dq1 * (-1.0) * 2.0
    y = dz1 + f64(old)
    return y

@@ -1,0 +1,156 @@
+from contextlib import ExitStack
+
+import concourse.mybir as mybir
+
+G, D, M, N = 4, 128, 128, 512
+P = 128
+PACK = 4
+ROWS = D // PACK
+FLOPS = 3 * 2 * G * D * M * N
+
+F32 = mybir.dt.float32
+BF16 = mybir.dt.bfloat16
+U32 = mybir.dt.uint32
+U8 = mybir.dt.uint8
+FP8X4 = mybir.dt.float8_e4m3fn_x4
+ALU = mybir.AluOpType
+ACT = mybir.ActivationFunctionType
+
+VECTOR_COLUMNS = 336
+
+
+def interleave_views(packed, raw, lo, hi):
+    dst = packed[:, lo:hi, :].rearrange("p (c i) j -> p c j i", i=PACK)
+    src = raw[:, :, lo:hi].rearrange("p j (c i) -> p c j i", i=PACK)
+    return dst, src
+
+
+def tile_rows_bkernrbf_kernel(tc, x, w1, w2, sh, d0, wo, dy, old, out):
+    nc = tc.nc
+    with ExitStack() as ctx:
+        sb = ctx.enter_context(tc.tile_pool(name="sb", bufs=1))
+        ps = ctx.enter_context(tc.psum_pool(name="ps", bufs=1))
+        ctx.enter_context(tc.manual_schedule())
+
+        def operand(name, width):
+            raw = sb.tile([P, PACK, width], F32, name=name + "_raw")
+            packed = sb.tile([P, width, PACK], BF16, name=name + "_packed", align_bytes=64)
+            codes = sb.tile([P, width], U32, name=name + "_codes", align_bytes=64)
+            scales = sb.tile([P, width], U8, name=name + "_scales", align_bytes=64)
+            return raw, packed, codes, scales
+
+        def load_operand(op, src):
+            nc.sync.dma_start(out=op[0][:], in_=src.rearrange("g (p j) c -> (g p) j c", j=PACK))
+
+        def pack_vector(op, lo, hi):
+            dst, src = interleave_views(op[1], op[0], lo, hi)
+            nc.vector.tensor_copy(out=dst, in_=src)
+
+        def pack_scalar(op, lo, hi):
+            dst, src = interleave_views(op[1], op[0], lo, hi)
+            nc.scalar.copy(out=dst, in_=src)
+
+        def quantize(op):
+            nc.vector.quantize_mx(out=op[2][:].bitcast(FP8X4), scales=op[3][:], in_=op[1][:].rearrange("p c j -> p (c j)"))
+
+        def product(bank, weights, columns, g):
+            rows = slice(ROWS * g, ROWS * (g + 1))
+            nc.tensor.matmul_mx(
+                out=bank[:],
+                lhsT=weights[2][rows, :].bitcast(FP8X4),
+                lhsT_scale=weights[3][rows, :],
+                rhs=columns[2][rows, :].bitcast(FP8X4),
+                rhs_scale=columns[3][rows, :],
+                start=True,
+                stop=True,
+            )
+
+        xo, dyo = operand("x", N), operand("dy", N)
+        w1o, w2o, woo = operand("w1", M), operand("w2", M), operand("wo", M)
+        d0_sb = [sb.tile([P, N], F32, name="d0_%d" % g) for g in range(G)]
+        old_sb = [sb.tile([P, N], F32, name="old_%d" % g) for g in range(G)]
+        arg = [sb.tile([P, N], F32, name="arg_%d" % g) for g in range(G)]
+        gauss = [sb.tile([P, N], F32, name="gauss_%d" % g) for g in range(G)]
+        weighted = [sb.tile([P, N], F32, name="weighted_%d" % g) for g in range(G)]
+        grad = [sb.tile([P, N], F32, name="grad_%d" % g) for g in range(G)]
+        res = [sb.tile([P, N], F32, name="res_%d" % g) for g in range(G)]
+        bank_a = [ps.tile([P, N], F32, name="bank_a%d" % g) for g in range(G)]
+        bank_b = [ps.tile([P, N], F32, name="bank_b%d" % g) for g in range(G)]
+        sh_rows = sb.tile([P, P], F32, name="sh_rows", align_bytes=64)
+        sh_cols = sb.tile([P, P], F32, name="sh_cols", align_bytes=64)
+
+        nc.gpsimd.memset(sh_rows[:], 0.0)
+        nc.scalar.dma_start(
+            out=sh_rows[0:P:32, :].rearrange("q (g i) -> q g i", i=32),
+            in_=sh.rearrange("g (q i) one -> q g (i one)", i=32),
+        )
+        load_operand(xo, x)
+        load_operand(w1o, w1)
+        nc.sync.dma_start(out=d0_sb[0][:], in_=d0[0])
+        load_operand(w2o, w2)
+        nc.sync.dma_start(out=d0_sb[1][:], in_=d0[1])
+        load_operand(woo, wo)
+        load_operand(dyo, dy)
+        nc.sync.dma_start(out=d0_sb[2][:], in_=d0[2])
+        nc.sync.dma_start(out=d0_sb[3][:], in_=d0[3])
+        for g in range(G):
+            nc.sync.dma_start(out=old_sb[g][:], in_=old[g])
+
+        def sharp(g):
+            return sh_cols[:, 32 * g : 32 * g + 1]
+
+        def step_arg(g):
+            nc.vector.scalar_tensor_tensor(out=arg[g][:], in0=bank_a[g][:], scalar=2.0, in1=d0_sb[g][:], op0=ALU.mult, op1=ALU.subtract)
+            nc.scalar.activation(out=gauss[g][:], in_=arg[g][:], func=ACT.Exp, scale=sharp(g))
+
+        def step_weight(g):
+            nc.vector.scalar_tensor_tensor(out=weighted[g][:], in0=bank_b[g][:], scalar=sharp(g), in1=gauss[g][:], op0=ALU.mult, op1=ALU.mult)
+
+        def step_grad(g):
+            nc.vector.scalar_tensor_tensor(out=grad[g][:], in0=bank_a[g][:], scalar=2.0, in1=weighted[g][:], op0=ALU.mult, op1=ALU.mult)
+
+        def step_out(g, engine):
+            engine.tensor_tensor(out=res[g][:], in0=grad[g][:], in1=old_sb[g][:], op=ALU.add)
+            nc.sync.dma_start(out=out[g], in_=res[g][:])
+
+        nc.vector.transpose(sh_cols[:], sh_rows[:])
+        pack_vector(xo, 0, VECTOR_COLUMNS)
+        pack_scalar(xo, VECTOR_COLUMNS, N)
+        pack_scalar(w1o, 0, M)
+        quantize(xo)
+        quantize(w1o)
+        product(bank_a[0], w1o, xo, 0)
+        product(bank_a[1], w1o, xo, 1)
+        pack_vector(w2o, 0, M)
+        pack_scalar(woo, 0, M)
+        step_arg(0)
+        quantize(w2o)
+        product(bank_b[0], w2o, xo, 0)
+        product(bank_b[1], w2o, xo, 1)
+        for g in range(2, G):
+            product(bank_a[g], w1o, xo, g)
+        for g in range(2, G):
+            product(bank_b[g], w2o, xo, g)
+        step_arg(1)
+        step_weight(0)
+        quantize(woo)
+        step_weight(1)
+        pack_vector(dyo, 0, VECTOR_COLUMNS)
+        pack_scalar(dyo, VECTOR_COLUMNS, N)
+        quantize(dyo)
+        product(bank_a[0], woo, dyo, 0)
+        product(bank_a[1], woo, dyo, 1)
+        step_arg(2)
+        product(bank_a[2], woo, dyo, 2)
+        step_grad(0)
+        step_out(0, nc.gpsimd)
+        step_grad(1)
+        step_out(1, nc.gpsimd)
+        step_arg(3)
+        product(bank_a[3], woo, dyo, 3)
+        step_weight(2)
+        step_grad(2)
+        step_out(2, nc.gpsimd)
+        step_weight(3)
+        step_grad(3)
+        step_out(3, nc.vector)

@@ -16,7 +16,9 @@ FP8X4 = mybir.dt.float8_e4m3fn_x4
 ALU = mybir.AluOpType
 ACT = mybir.ActivationFunctionType
 
-VECTOR_COLUMNS = 336
+X_VECTOR_COLUMNS = 400
+DY_VECTOR_COLUMNS = 352
+HALF = N // 2
 
 
 def interleave_views(packed, raw, lo, hi):
@@ -50,8 +52,12 @@ def tile_rows_bkernrbf_kernel(tc, x, w1, w2, sh, d0, wo, dy, old, out):
             dst, src = interleave_views(op[1], op[0], lo, hi)
             nc.scalar.copy(out=dst, in_=src)
 
-        def quantize(op):
-            nc.vector.quantize_mx(out=op[2][:].bitcast(FP8X4), scales=op[3][:], in_=op[1][:].rearrange("p c j -> p (c j)"))
+        def quantize(op, lo, hi):
+            nc.vector.quantize_mx(
+                out=op[2][:, lo:hi].bitcast(FP8X4),
+                scales=op[3][:, lo:hi],
+                in_=op[1][:, lo:hi, :].rearrange("p c j -> p (c j)"),
+            )
 
         def product(bank, weights, columns, g):
             rows = slice(ROWS * g, ROWS * (g + 1))
@@ -74,33 +80,40 @@ def tile_rows_bkernrbf_kernel(tc, x, w1, w2, sh, d0, wo, dy, old, out):
         weighted = [sb.tile([P, N], F32, name="weighted_%d" % g) for g in range(G)]
         grad = [sb.tile([P, N], F32, name="grad_%d" % g) for g in range(G)]
         res = [sb.tile([P, N], F32, name="res_%d" % g) for g in range(G)]
+        doubled = {g: sb.tile([P, N], F32, name="doubled_%d" % g) for g in (2, 3)}
         bank_a = [ps.tile([P, N], F32, name="bank_a%d" % g) for g in range(G)]
         bank_b = [ps.tile([P, N], F32, name="bank_b%d" % g) for g in range(G)]
         sh_rows = sb.tile([P, P], F32, name="sh_rows", align_bytes=64)
         sh_cols = sb.tile([P, P], F32, name="sh_cols", align_bytes=64)
 
         nc.gpsimd.memset(sh_rows[:], 0.0)
-        nc.scalar.dma_start(
+        load_operand(w1o, w1)
+        nc.sync.dma_start(
             out=sh_rows[0:P:32, :].rearrange("q (g i) -> q g i", i=32),
             in_=sh.rearrange("g (q i) one -> q g (i one)", i=32),
         )
         load_operand(xo, x)
-        load_operand(w1o, w1)
-        nc.sync.dma_start(out=d0_sb[0][:], in_=d0[0])
-        load_operand(w2o, w2)
-        nc.sync.dma_start(out=d0_sb[1][:], in_=d0[1])
-        load_operand(woo, wo)
         load_operand(dyo, dy)
-        nc.sync.dma_start(out=d0_sb[2][:], in_=d0[2])
-        nc.sync.dma_start(out=d0_sb[3][:], in_=d0[3])
+        load_operand(woo, wo)
+        load_operand(w2o, w2)
+        for g in range(G):
+            nc.sync.dma_start(out=d0_sb[g][:], in_=d0[g])
         for g in range(G):
             nc.sync.dma_start(out=old_sb[g][:], in_=old[g])
 
         def sharp(g):
             return sh_cols[:, 32 * g : 32 * g + 1]
 
-        def step_arg(g):
+        def arg_vector(g):
             nc.vector.scalar_tensor_tensor(out=arg[g][:], in0=bank_a[g][:], scalar=2.0, in1=d0_sb[g][:], op0=ALU.mult, op1=ALU.subtract)
+
+        def double_out(g):
+            nc.scalar.activation(out=doubled[g][:], in_=bank_a[g][:], func=ACT.Copy, scale=2.0)
+
+        def arg_gpsimd(g):
+            nc.gpsimd.tensor_tensor(out=arg[g][:], in0=doubled[g][:], in1=d0_sb[g][:], op=ALU.subtract)
+
+        def step_exp(g):
             nc.scalar.activation(out=gauss[g][:], in_=arg[g][:], func=ACT.Exp, scale=sharp(g))
 
         def step_weight(g):
@@ -109,48 +122,55 @@ def tile_rows_bkernrbf_kernel(tc, x, w1, w2, sh, d0, wo, dy, old, out):
         def step_grad(g):
             nc.vector.scalar_tensor_tensor(out=grad[g][:], in0=bank_a[g][:], scalar=2.0, in1=weighted[g][:], op0=ALU.mult, op1=ALU.mult)
 
-        def step_out(g, engine):
-            engine.tensor_tensor(out=res[g][:], in0=grad[g][:], in1=old_sb[g][:], op=ALU.add)
-            nc.sync.dma_start(out=out[g], in_=res[g][:])
+        def step_out(g, engine, lo, hi):
+            engine.tensor_tensor(out=res[g][:, lo:hi], in0=grad[g][:, lo:hi], in1=old_sb[g][:, lo:hi], op=ALU.add)
+            nc.sync.dma_start(out=out[g][:, lo:hi], in_=res[g][:, lo:hi])
 
+        pack_vector(w1o, 0, M)
         nc.vector.transpose(sh_cols[:], sh_rows[:])
-        pack_vector(xo, 0, VECTOR_COLUMNS)
-        pack_scalar(xo, VECTOR_COLUMNS, N)
-        pack_scalar(w1o, 0, M)
-        quantize(xo)
-        quantize(w1o)
-        product(bank_a[0], w1o, xo, 0)
-        product(bank_a[1], w1o, xo, 1)
-        pack_vector(w2o, 0, M)
-        pack_scalar(woo, 0, M)
-        step_arg(0)
-        quantize(w2o)
-        product(bank_b[0], w2o, xo, 0)
-        product(bank_b[1], w2o, xo, 1)
-        for g in range(2, G):
+        quantize(w1o, 0, M)
+        pack_vector(xo, 0, HALF)
+        pack_vector(xo, HALF, X_VECTOR_COLUMNS)
+        pack_scalar(xo, X_VECTOR_COLUMNS, N)
+        quantize(xo, 0, HALF)
+        quantize(xo, HALF, N)
+        for g in range(G):
             product(bank_a[g], w1o, xo, g)
-        for g in range(2, G):
-            product(bank_b[g], w2o, xo, g)
-        step_arg(1)
+        pack_vector(dyo, 0, HALF)
+        pack_vector(dyo, HALF, DY_VECTOR_COLUMNS)
+        pack_scalar(dyo, DY_VECTOR_COLUMNS, N)
+        pack_scalar(woo, 0, M)
+        pack_scalar(w2o, 0, M)
+        quantize(dyo, 0, HALF)
+        quantize(dyo, HALF, N)
+        quantize(woo, 0, M)
+        for g in range(G):
+            product(bank_b[g], woo, dyo, g)
+        arg_vector(0)
+        double_out(2)
+        step_exp(0)
+        quantize(w2o, 0, M)
+        product(bank_a[0], w2o, xo, 0)
+        product(bank_a[2], w2o, xo, 2)
+        arg_vector(1)
+        product(bank_a[1], w2o, xo, 1)
+        arg_gpsimd(2)
+        double_out(3)
+        product(bank_a[3], w2o, xo, 3)
+        step_exp(1)
+        step_exp(2)
+        arg_gpsimd(3)
+        step_exp(3)
         step_weight(0)
-        quantize(woo)
-        step_weight(1)
-        pack_vector(dyo, 0, VECTOR_COLUMNS)
-        pack_scalar(dyo, VECTOR_COLUMNS, N)
-        quantize(dyo)
-        product(bank_a[0], woo, dyo, 0)
-        product(bank_a[1], woo, dyo, 1)
-        step_arg(2)
-        product(bank_a[2], woo, dyo, 2)
         step_grad(0)
-        step_out(0, nc.gpsimd)
-        step_grad(1)
-        step_out(1, nc.gpsimd)
-        step_arg(3)
-        product(bank_a[3], woo, dyo, 3)
+        step_out(0, nc.gpsimd, 0, N)
+        step_weight(1)
         step_weight(2)
-        step_grad(2)
-        step_out(2, nc.gpsimd)
+        step_grad(1)
+        step_out(1, nc.gpsimd, 0, N)
         step_weight(3)
+        step_grad(2)
         step_grad(3)
-        step_out(3, nc.vector)
+        step_out(2, nc.vector, 0, N)
+        step_out(3, nc.vector, 0, HALF)
+        step_out(3, nc.vector, HALF, N)

from contextlib import ExitStack

import concourse.mybir as mybir

G, D, M, N = 4, 128, 128, 512
P = 128
PACK = 4
ROWS = D // PACK
FLOPS = 3 * 2 * G * D * M * N

F32 = mybir.dt.float32
BF16 = mybir.dt.bfloat16
U32 = mybir.dt.uint32
U8 = mybir.dt.uint8
FP8X4 = mybir.dt.float8_e4m3fn_x4
ALU = mybir.AluOpType
ACT = mybir.ActivationFunctionType

X_VECTOR_COLUMNS = 400
DY_VECTOR_COLUMNS = 352
HALF = N // 2


def interleave_views(packed, raw, lo, hi):
    dst = packed[:, lo:hi, :].rearrange("p (c i) j -> p c j i", i=PACK)
    src = raw[:, :, lo:hi].rearrange("p j (c i) -> p c j i", i=PACK)
    return dst, src


def tile_rows_bkernrbf_kernel(tc, x, w1, w2, sh, d0, wo, dy, old, out):
    nc = tc.nc
    with ExitStack() as ctx:
        sb = ctx.enter_context(tc.tile_pool(name="sb", bufs=1))
        ps = ctx.enter_context(tc.psum_pool(name="ps", bufs=1))
        ctx.enter_context(tc.manual_schedule())

        def operand(name, width):
            raw = sb.tile([P, PACK, width], F32, name=name + "_raw")
            packed = sb.tile([P, width, PACK], BF16, name=name + "_packed", align_bytes=64)
            codes = sb.tile([P, width], U32, name=name + "_codes", align_bytes=64)
            scales = sb.tile([P, width], U8, name=name + "_scales", align_bytes=64)
            return raw, packed, codes, scales

        def load_operand(op, src):
            nc.sync.dma_start(out=op[0][:], in_=src.rearrange("g (p j) c -> (g p) j c", j=PACK))

        def pack_vector(op, lo, hi):
            dst, src = interleave_views(op[1], op[0], lo, hi)
            nc.vector.tensor_copy(out=dst, in_=src)

        def pack_scalar(op, lo, hi):
            dst, src = interleave_views(op[1], op[0], lo, hi)
            nc.scalar.copy(out=dst, in_=src)

        def quantize(op, lo, hi):
            nc.vector.quantize_mx(
                out=op[2][:, lo:hi].bitcast(FP8X4),
                scales=op[3][:, lo:hi],
                in_=op[1][:, lo:hi, :].rearrange("p c j -> p (c j)"),
            )

        def product(bank, weights, columns, g):
            rows = slice(ROWS * g, ROWS * (g + 1))
            nc.tensor.matmul_mx(
                out=bank[:],
                lhsT=weights[2][rows, :].bitcast(FP8X4),
                lhsT_scale=weights[3][rows, :],
                rhs=columns[2][rows, :].bitcast(FP8X4),
                rhs_scale=columns[3][rows, :],
                start=True,
                stop=True,
            )

        xo, dyo = operand("x", N), operand("dy", N)
        w1o, w2o, woo = operand("w1", M), operand("w2", M), operand("wo", M)
        d0_sb = [sb.tile([P, N], F32, name="d0_%d" % g) for g in range(G)]
        old_sb = [sb.tile([P, N], F32, name="old_%d" % g) for g in range(G)]
        arg = [sb.tile([P, N], F32, name="arg_%d" % g) for g in range(G)]
        gauss = [sb.tile([P, N], F32, name="gauss_%d" % g) for g in range(G)]
        weighted = [sb.tile([P, N], F32, name="weighted_%d" % g) for g in range(G)]
        grad = [sb.tile([P, N], F32, name="grad_%d" % g) for g in range(G)]
        res = [sb.tile([P, N], F32, name="res_%d" % g) for g in range(G)]
        doubled = {g: sb.tile([P, N], F32, name="doubled_%d" % g) for g in (2, 3)}
        bank_a = [ps.tile([P, N], F32, name="bank_a%d" % g) for g in range(G)]
        bank_b = [ps.tile([P, N], F32, name="bank_b%d" % g) for g in range(G)]
        sh_rows = sb.tile([P, P], F32, name="sh_rows", align_bytes=64)
        sh_cols = sb.tile([P, P], F32, name="sh_cols", align_bytes=64)

        nc.gpsimd.memset(sh_rows[:], 0.0)
        load_operand(w1o, w1)
        nc.sync.dma_start(
            out=sh_rows[0:P:32, :].rearrange("q (g i) -> q g i", i=32),
            in_=sh.rearrange("g (q i) one -> q g (i one)", i=32),
        )
        load_operand(xo, x)
        load_operand(dyo, dy)
        load_operand(woo, wo)
        load_operand(w2o, w2)
        for g in range(G):
            nc.sync.dma_start(out=d0_sb[g][:], in_=d0[g])
        for g in range(G):
            nc.sync.dma_start(out=old_sb[g][:], in_=old[g])

        def sharp(g):
            return sh_cols[:, 32 * g : 32 * g + 1]

        def arg_vector(g):
            nc.vector.scalar_tensor_tensor(out=arg[g][:], in0=bank_a[g][:], scalar=2.0, in1=d0_sb[g][:], op0=ALU.mult, op1=ALU.subtract)

        def double_out(g):
            nc.scalar.activation(out=doubled[g][:], in_=bank_a[g][:], func=ACT.Copy, scale=2.0)

        def arg_gpsimd(g):
            nc.gpsimd.tensor_tensor(out=arg[g][:], in0=doubled[g][:], in1=d0_sb[g][:], op=ALU.subtract)

        def step_exp(g):
            nc.scalar.activation(out=gauss[g][:], in_=arg[g][:], func=ACT.Exp, scale=sharp(g))

        def step_weight(g):
            nc.vector.scalar_tensor_tensor(out=weighted[g][:], in0=bank_b[g][:], scalar=sharp(g), in1=gauss[g][:], op0=ALU.mult, op1=ALU.mult)

        def step_grad(g):
            nc.vector.scalar_tensor_tensor(out=grad[g][:], in0=bank_a[g][:], scalar=2.0, in1=weighted[g][:], op0=ALU.mult, op1=ALU.mult)

        def step_out(g, engine, lo, hi):
            engine.tensor_tensor(out=res[g][:, lo:hi], in0=grad[g][:, lo:hi], in1=old_sb[g][:, lo:hi], op=ALU.add)
            nc.sync.dma_start(out=out[g][:, lo:hi], in_=res[g][:, lo:hi])

        pack_vector(w1o, 0, M)
        nc.vector.transpose(sh_cols[:], sh_rows[:])
        quantize(w1o, 0, M)
        pack_vector(xo, 0, HALF)
        pack_vector(xo, HALF, X_VECTOR_COLUMNS)
        pack_scalar(xo, X_VECTOR_COLUMNS, N)
        quantize(xo, 0, HALF)
        quantize(xo, HALF, N)
        for g in range(G):
            product(bank_a[g], w1o, xo, g)
        pack_vector(dyo, 0, HALF)
        pack_vector(dyo, HALF, DY_VECTOR_COLUMNS)
        pack_scalar(dyo, DY_VECTOR_COLUMNS, N)
        pack_scalar(woo, 0, M)
        pack_scalar(w2o, 0, M)
        quantize(dyo, 0, HALF)
        quantize(dyo, HALF, N)
        quantize(woo, 0, M)
        for g in range(G):
            product(bank_b[g], woo, dyo, g)
        arg_vector(0)
        double_out(2)
        step_exp(0)
        quantize(w2o, 0, M)
        product(bank_a[0], w2o, xo, 0)
        product(bank_a[2], w2o, xo, 2)
        arg_vector(1)
        product(bank_a[1], w2o, xo, 1)
        arg_gpsimd(2)
        double_out(3)
        product(bank_a[3], w2o, xo, 3)
        step_exp(1)
        step_exp(2)
        arg_gpsimd(3)
        step_exp(3)
        step_weight(0)
        step_grad(0)
        step_out(0, nc.gpsimd, 0, N)
        step_weight(1)
        step_weight(2)
        step_grad(1)
        step_out(1, nc.gpsimd, 0, N)
        step_weight(3)
        step_grad(2)
        step_grad(3)
        step_out(2, nc.vector, 0, N)
        step_out(3, nc.vector, 0, HALF)
        step_out(3, nc.vector, HALF, N)
